import numpy as np
import ml_dtypes


def mxq(x, axis, fmt="e4m3"):
    dtype, down = {"e4m3": (ml_dtypes.float8_e4m3fn, 7), "e5m2": (ml_dtypes.float8_e5m2, 14)}[fmt]
    v = np.moveaxis(np.asarray(x, np.float32).astype(ml_dtypes.bfloat16).astype(np.float64), axis, -1)
    blocks = v.reshape(v.shape[:-1] + (-1, 32))
    amax = np.abs(blocks).max(-1, keepdims=True)
    byte = np.maximum(np.where(amax > 0, np.frexp(amax)[1] - 1 + 127, 0) - down, 1)
    scale = np.exp2(byte - 127.0)
    codes = (blocks / scale).astype(np.float32).astype(dtype).astype(np.float64)
    return np.moveaxis((codes * scale).reshape(v.shape), -1, axis)


WIDE = False


def mx_kscale(k):
    if not WIDE:
        return np.ones(k)
    levels = np.array([10, -10, 5, -5, 0])
    if k % 512:
        return np.exp2(np.random.permutation(np.resize(levels, k // 32))).repeat(32)
    a = np.empty((k // 512, 16))
    for p in range(k // 512):
        a[p, :8] = np.random.permutation(np.resize(levels, 8))
        for g in range(8):
            far = levels[np.abs(levels - a[p, g]) >= 10]
            a[p, g + 8] = far[np.random.randint(len(far))]
    return np.exp2(a.ravel()).repeat(32)


def f64(x):
    return np.asarray(x).astype(np.float64)


def striped(idx):
    return np.tile(idx.reshape(-1, 16).T, (8, 1)).astype(np.uint16)


def unstriped(offs):
    return offs[:16].T.reshape(-1).astype(np.int64)


E2M1 = np.array([0.0, 0.5, 1.0, 1.5, 2.0, 3.0, 4.0, 6.0, -0.0, -0.5, -1.0, -1.5, -2.0, -3.0, -4.0, -6.0])


def pack_fp4(w):
    k, n = w.shape
    w = f64(np.asarray(w, np.float32).astype(ml_dtypes.bfloat16)).reshape(k // 32, 32, n)
    amax = np.abs(w).max(1)
    mant, ex = np.frexp(amax / 6.0)
    byte = np.clip(np.where(amax > 0, np.where(mant > 0.5, ex, ex - 1) + 127, 1), 1, 254)
    scaled = (w * np.exp2(127.0 - byte)[:, None, :]).reshape(k, n).astype(np.float32)
    c = np.ascontiguousarray(scaled.reshape(k // 512, 128, 4, n).transpose(0, 1, 3, 2)).astype(ml_dtypes.float4_e2m1fn).view(np.uint8) & 0xF
    words = (c[..., 0::2] | (c[..., 1::2] << 4)).reshape(k // 512, 128, 2 * n)
    return np.ascontiguousarray(words), np.ascontiguousarray(byte.astype(np.uint8).reshape(k // 512, 16, n))


def unpack_fp4(words, scales):
    g, _, n = scales.shape
    words = np.ascontiguousarray(words).reshape(g, 128, n, 2)
    nib = np.empty((g, 128, n, 4), np.uint8)
    nib[..., 0::2] = words & 0xF
    nib[..., 1::2] = words >> 4
    vals = E2M1[nib] * np.repeat(np.exp2(scales.astype(np.float64) - 127.0), 8, axis=1)[..., None]
    return vals.transpose(0, 1, 3, 2).reshape(g * 512, n)


K, T, S, N = 512, 4096, 1024, 256


def setup_inputs():
    n = np.random.standard_normal
    s = mx_kscale(K)[:, None]
    packed_w1 = pack_fp4(n((K, N)) / np.sqrt(K) / s)
    packed_w2 = pack_fp4(n((K, N)) / np.sqrt(K) / s)
    packed_w3 = pack_fp4(n((K, N)) / np.sqrt(K) / s)
    return {
        "xT": (n((K, T)) * s).astype(np.float32),
        "w1_words": packed_w1[0],
        "w1_scales": packed_w1[1],
        "w2_words": packed_w2[0],
        "w2_scales": packed_w2[1],
        "w3_words": packed_w3[0],
        "w3_scales": packed_w3[1],
        "offs": striped(np.random.permutation(T)[:S]),
    }


def reference(xT, w1_words, w1_scales, w2_words, w2_scales, w3_words, w3_scales, offs):
    xq = mxq(f64(xT)[:, unstriped(offs)], 0, "e4m3")
    return np.minimum(np.minimum(unpack_fp4(w1_words, w1_scales).T @ xq, unpack_fp4(w2_words, w2_scales).T @ xq), unpack_fp4(w3_words, w3_scales).T @ xq)

@@ -1,0 +1,143 @@
+from contextlib import ExitStack
+
+import concourse.mybir as mybir
+
+K, T, S, N = 512, 4096, 1024, 256
+FLOPS = 2 * 3 * K * N * S
+
+F32 = mybir.dt.float32
+BF16 = mybir.dt.bfloat16
+I32 = mybir.dt.int32
+U32 = mybir.dt.uint32
+U16 = mybir.dt.uint16
+U8 = mybir.dt.uint8
+FP8X4 = mybir.dt.float8_e4m3fn_x4
+FP4X4 = mybir.dt.float4_e2m1fn_x4
+COPY = mybir.ActivationFunctionType.Copy
+MIN = mybir.AluOpType.min
+
+P = 128
+PACK = 4
+HALF = S // 2
+UNIT = 256
+M_TILES = N // P
+LAST_CHUNKS = [[1536,"s"],[1024,"s"],[1024,"v"],[512,"s"]]
+SPLIT = True
+
+
+def tile_picked_maxout_min_e_kernel(tc, xT, w1_words, w1_scales, w2_words, w2_scales, w3_words, w3_scales, offs, out):
+    nc = tc.nc
+    x_planes = xT.rearrange("(p j) t -> p j t", j=PACK)
+    out_view = out.rearrange("(mt p) s -> p mt s", p=P)
+
+    with ExitStack() as ctx:
+        keep = ctx.enter_context(tc.tile_pool(name="keep", bufs=1))
+        psum = ctx.enter_context(tc.psum_pool(name="psum", bufs=1))
+
+        offsets = keep.tile([P, S // 16], U16, name="offsets")
+        planes = [keep.tile([P, T], F32, name="plane%d" % j) for j in range(PACK)]
+        last_bf = keep.tile([P, T], BF16, name="last_bf")
+        grouped = [keep.tile([P, HALF, PACK], BF16, name="grouped%d" % h, align_bytes=64) for h in range(2)]
+        w_words = [keep.tile([P, 2 * N], U8, name="w_words%d" % i, align_bytes=64) for i in range(3)]
+        w_scales = keep.tile([P, 3 * N], U8, name="w_scales", align_bytes=64)
+        scale_rows = keep.tile([16, 3 * N], U8, name="scale_rows")
+        nc.gpsimd.memset(w_scales[:].bitcast(I32), 0)
+        for i, scales in enumerate((w1_scales, w2_scales, w3_scales)):
+            nc.scalar.dma_start(scale_rows[:, i * N : (i + 1) * N].bitcast(I32), scales[0].bitcast(I32))
+        for q in range(4):
+            nc.gpsimd.dma_start(w_scales[32 * q : 32 * q + 4, :].bitcast(I32), scale_rows[4 * q : 4 * q + 4, :].bitcast(I32))
+
+        nc.sync.dma_start(planes[0][:], x_planes[:, 0, :])
+        nc.sync.dma_start(offsets[:], offs)
+        for j in range(1, PACK - 1):
+            nc.sync.dma_start(planes[j][:], x_planes[:, j, :])
+        c0 = 0
+        bounds = []
+        for width, eng in LAST_CHUNKS:
+            nc.sync.dma_start(planes[PACK - 1][:, c0 : c0 + width], x_planes[:, PACK - 1, c0 : c0 + width])
+            bounds.append((c0, c0 + width, eng))
+            c0 = c0 + width
+        for i, words in enumerate((w1_words, w2_words, w3_words)):
+            nc.sync.dma_start(w_words[i][:].bitcast(I32), words[0].bitcast(I32))
+
+        def half_offsets(h):
+            return offsets[:, h * (HALF // 16) : (h + 1) * (HALF // 16)]
+
+        for j in range(PACK - 1):
+            for h in range(2):
+                nc.vector.tensor_copy(grouped[h][:, :, j], planes[j][:].indirect(half_offsets(h)))
+
+        j = PACK - 1
+        if SPLIT:
+            for a, b, eng in bounds:
+                if eng == "s":
+                    nc.scalar.activation(last_bf[:, a:b], planes[j][:, a:b], COPY)
+                else:
+                    nc.vector.tensor_copy(last_bf[:, a:b], planes[j][:, a:b])
+        nc.vector.tensor_copy(grouped[0][:, :, j], planes[j][:].indirect(half_offsets(0)))
+        if SPLIT:
+            nc.scalar.activation(grouped[1][:, :, j], last_bf[:].indirect(half_offsets(1)), COPY)
+
+        units = S // UNIT
+        codes = [keep.tile([P, UNIT], U32, name="codes%d" % u, align_bytes=64) for u in range(units)]
+        x_scales = [keep.tile([P, UNIT], U8, name="x_scales%d" % u, align_bytes=64) for u in range(units)]
+        width = M_TILES * UNIT
+        first = keep.tile([P, units * width], F32, name="last_bf")
+        pair = keep.tile([P, units * width], F32, name="grouped1", align_bytes=64)
+        result = [keep.tile([P, M_TILES, UNIT], F32, name="result%d" % u) for u in range(units)]
+        banks = {}
+
+        def quantise(u):
+            h, r = divmod(u * UNIT, HALF)
+            nc.vector.quantize_mx(
+                out=codes[u][:].bitcast(FP8X4),
+                scales=x_scales[u][:],
+                in_=grouped[h][:, r : r + UNIT, :].rearrange("p n j -> p (n j)"),
+            )
+
+        def products(u):
+            for i in range(3):
+                acc = psum.tile([P, M_TILES * UNIT], F32, name="acc%d" % i, bufs=(2, 3, 3)[i])
+                for mt in range(M_TILES):
+                    nc.tensor.matmul_mx(
+                        out=acc[:, mt * UNIT : (mt + 1) * UNIT],
+                        lhsT=w_words[i][:, 2 * P * mt : 2 * P * (mt + 1)].bitcast(FP4X4),
+                        lhsT_scale=w_scales[:, i * N + P * mt : i * N + P * (mt + 1)],
+                        rhs=codes[u][:].bitcast(FP8X4),
+                        rhs_scale=x_scales[u][:],
+                        start=True,
+                        stop=True,
+                    )
+                banks[(u, i)] = acc
+            nc.scalar.copy(first[:, u * width : (u + 1) * width], banks[(u, 0)][:])
+
+        def min_two(u):
+            nc.vector.tensor_tensor(pair[:, u * width : (u + 1) * width], banks[(u, 1)][:], first[:, u * width : (u + 1) * width], MIN)
+
+        def min_three(u):
+            cols = slice(u * UNIT, (u + 1) * UNIT)
+            if u < units - 1:
+                nc.vector.tensor_tensor(result[u][:].rearrange("p m n -> p (m n)"), banks[(u, 2)][:], pair[:, u * width : (u + 1) * width], MIN)
+                nc.sync.dma_start(out_view[:, :, cols], result[u][:])
+            else:
+                for mt in range(M_TILES):
+                    part = slice(mt * UNIT, (mt + 1) * UNIT)
+                    nc.vector.tensor_tensor(result[u][:, mt, :], banks[(u, 2)][:, part], pair[:, u * width + mt * UNIT : u * width + (mt + 1) * UNIT], MIN)
+                    nc.sync.dma_start(out_view[:, mt, cols], result[u][:, mt, :])
+
+        quantise(0)
+        quantise(1)
+        products(0)
+        products(1)
+        quantise(2)
+        quantise(3)
+        products(2)
+        min_two(0)
+        min_three(0)
+        products(3)
+        min_two(1)
+        min_two(2)
+        min_three(1)
+        min_two(3)
+        min_three(2)
+        min_three(3)

@@ -60,6 +60,13 @@ def tile_picked_maxout_min_e_kernel(tc, xT, w1_words, w1_scales, w2_words, w2_sc
         for i, words in enumerate((w1_words, w2_words, w3_words)):
             nc.sync.dma_start(w_words[i][:].bitcast(I32), words[0].bitcast(I32))
 
+        zeros = keep.tile([P, 2048], BF16, name="zeros", align_bytes=64)
+        warm_codes = keep.tile([P, 512], U32, name="warm_codes", align_bytes=64)
+        warm_scales = keep.tile([P, 512], U8, name="warm_scales", align_bytes=64)
+        warm_bank = psum.tile([P, 512], F32, name="acc2", bufs=3)
+        nc.vector.memset(zeros[:], 0.0)
+        nc.vector.quantize_mx(out=warm_codes[:].bitcast(FP8X4), scales=warm_scales[:], in_=zeros[:])
+
         def half_offsets(h):
             return offsets[:, h * (HALF // 16) : (h + 1) * (HALF // 16)]
 
@@ -125,6 +132,16 @@ def tile_picked_maxout_min_e_kernel(tc, xT, w1_words, w1_scales, w2_words, w2_sc
                     nc.vector.tensor_tensor(result[u][:, mt, :], banks[(u, 2)][:, part], pair[:, u * width + mt * UNIT : u * width + (mt + 1) * UNIT], MIN)
                     nc.sync.dma_start(out_view[:, mt, cols], result[u][:, mt, :])
 
+        for r in range(3):
+            nc.tensor.matmul_mx(
+                out=warm_bank[:],
+                lhsT=w_words[0][:, 0 : 2 * P].bitcast(FP4X4),
+                lhsT_scale=w_scales[:, 0:P],
+                rhs=warm_codes[:].bitcast(FP8X4),
+                rhs_scale=warm_scales[:],
+                start=True,
+                stop=True,
+            )
         quantise(0)
         quantise(1)
         products(0)

@@ -21,7 +21,7 @@ PACK = 4
 HALF = S // 2
 UNIT = 256
 M_TILES = N // P
-LAST_CHUNKS = [[1536,"s"],[1024,"s"],[1024,"v"],[512,"s"]]
+LAST_CHUNKS = [[1536,"s"],[1024,"s"],[1024,"v"],[256,"s"],[256,"s"]]
 SPLIT = True
 
 
@@ -102,8 +102,8 @@ def tile_picked_maxout_min_e_kernel(tc, xT, w1_words, w1_scales, w2_words, w2_sc
                 in_=grouped[h][:, r : r + UNIT, :].rearrange("p n j -> p (n j)"),
             )
 
-        def products(u):
-            for i in range(3):
+        def product(u, i):
+            if True:
                 acc = psum.tile([P, M_TILES * UNIT], F32, name="acc%d" % i, bufs=(2, 3, 3)[i])
                 for mt in range(M_TILES):
                     nc.tensor.matmul_mx(
@@ -116,21 +116,15 @@ def tile_picked_maxout_min_e_kernel(tc, xT, w1_words, w1_scales, w2_words, w2_sc
                         stop=True,
                     )
                 banks[(u, i)] = acc
-            nc.scalar.copy(first[:, u * width : (u + 1) * width], banks[(u, 0)][:])
+            if i == 0:
+                nc.scalar.copy(first[:, u * width : (u + 1) * width], banks[(u, 0)][:])
 
-        def min_two(u):
-            nc.vector.tensor_tensor(pair[:, u * width : (u + 1) * width], banks[(u, 1)][:], first[:, u * width : (u + 1) * width], MIN)
+        def min_two(u, lo, hi):
+            nc.vector.tensor_tensor(pair[:, u * width + lo * UNIT : u * width + hi * UNIT], banks[(u, 1)][:, lo * UNIT : hi * UNIT], first[:, u * width + lo * UNIT : u * width + hi * UNIT], MIN)
 
-        def min_three(u):
-            cols = slice(u * UNIT, (u + 1) * UNIT)
-            if u < units - 1:
-                nc.vector.tensor_tensor(result[u][:].rearrange("p m n -> p (m n)"), banks[(u, 2)][:], pair[:, u * width : (u + 1) * width], MIN)
-                nc.sync.dma_start(out_view[:, :, cols], result[u][:])
-            else:
-                for mt in range(M_TILES):
-                    part = slice(mt * UNIT, (mt + 1) * UNIT)
-                    nc.vector.tensor_tensor(result[u][:, mt, :], banks[(u, 2)][:, part], pair[:, u * width + mt * UNIT : u * width + (mt + 1) * UNIT], MIN)
-                    nc.sync.dma_start(out_view[:, mt, cols], result[u][:, mt, :])
+        def min_three(u, lo, hi):
+            nc.vector.tensor_tensor(result[u][:, lo:hi, :].rearrange("p m n -> p (m n)"), banks[(u, 2)][:, lo * UNIT : hi * UNIT], pair[:, u * width + lo * UNIT : u * width + hi * UNIT], MIN)
+            nc.sync.dma_start(out_view[:, lo:hi, u * UNIT : (u + 1) * UNIT], result[u][:, lo:hi, :])
 
         for r in range(3):
             nc.tensor.matmul_mx(
@@ -144,17 +138,28 @@ def tile_picked_maxout_min_e_kernel(tc, xT, w1_words, w1_scales, w2_words, w2_sc
             )
         quantise(0)
         quantise(1)
-        products(0)
-        products(1)
         quantise(2)
         quantise(3)
-        products(2)
-        min_two(0)
-        min_three(0)
-        products(3)
-        min_two(1)
-        min_two(2)
-        min_three(1)
-        min_two(3)
-        min_three(2)
-        min_three(3)
+        product(0, 0)
+        product(0, 1)
+        product(1, 0)
+        product(1, 1)
+        product(0, 2)
+        product(2, 0)
+        product(2, 1)
+        product(1, 2)
+        min_two(0, 0, 2)
+        min_two(1, 0, 2)
+        product(3, 0)
+        product(3, 1)
+        product(2, 2)
+        min_three(0, 0, 2)
+        product(3, 2)
+        min_two(2, 0, 2)
+        min_three(1, 0, 2)
+        min_two(3, 0, 1)
+        min_three(2, 0, 1)
+        min_two(3, 1, 2)
+        min_three(2, 1, 2)
+        min_three(3, 0, 1)
+        min_three(3, 1, 2)

from contextlib import ExitStack

import concourse.mybir as mybir

K, T, S, N = 512, 4096, 1024, 256
FLOPS = 2 * 3 * K * N * S

F32 = mybir.dt.float32
BF16 = mybir.dt.bfloat16
I32 = mybir.dt.int32
U32 = mybir.dt.uint32
U16 = mybir.dt.uint16
U8 = mybir.dt.uint8
FP8X4 = mybir.dt.float8_e4m3fn_x4
FP4X4 = mybir.dt.float4_e2m1fn_x4
COPY = mybir.ActivationFunctionType.Copy
MIN = mybir.AluOpType.min

P = 128
PACK = 4
HALF = S // 2
UNIT = 256
M_TILES = N // P
LAST_CHUNKS = [[1536,"s"],[1024,"s"],[1024,"v"],[256,"s"],[256,"s"]]
SPLIT = True


def tile_picked_maxout_min_e_kernel(tc, xT, w1_words, w1_scales, w2_words, w2_scales, w3_words, w3_scales, offs, out):
    nc = tc.nc
    x_planes = xT.rearrange("(p j) t -> p j t", j=PACK)
    out_view = out.rearrange("(mt p) s -> p mt s", p=P)

    with ExitStack() as ctx:
        keep = ctx.enter_context(tc.tile_pool(name="keep", bufs=1))
        psum = ctx.enter_context(tc.psum_pool(name="psum", bufs=1))

        offsets = keep.tile([P, S // 16], U16, name="offsets")
        planes = [keep.tile([P, T], F32, name="plane%d" % j) for j in range(PACK)]
        last_bf = keep.tile([P, T], BF16, name="last_bf")
        grouped = [keep.tile([P, HALF, PACK], BF16, name="grouped%d" % h, align_bytes=64) for h in range(2)]
        w_words = [keep.tile([P, 2 * N], U8, name="w_words%d" % i, align_bytes=64) for i in range(3)]
        w_scales = keep.tile([P, 3 * N], U8, name="w_scales", align_bytes=64)
        scale_rows = keep.tile([16, 3 * N], U8, name="scale_rows")
        nc.gpsimd.memset(w_scales[:].bitcast(I32), 0)
        for i, scales in enumerate((w1_scales, w2_scales, w3_scales)):
            nc.scalar.dma_start(scale_rows[:, i * N : (i + 1) * N].bitcast(I32), scales[0].bitcast(I32))
        for q in range(4):
            nc.gpsimd.dma_start(w_scales[32 * q : 32 * q + 4, :].bitcast(I32), scale_rows[4 * q : 4 * q + 4, :].bitcast(I32))

        nc.sync.dma_start(planes[0][:], x_planes[:, 0, :])
        nc.sync.dma_start(offsets[:], offs)
        for j in range(1, PACK - 1):
            nc.sync.dma_start(planes[j][:], x_planes[:, j, :])
        c0 = 0
        bounds = []
        for width, eng in LAST_CHUNKS:
            nc.sync.dma_start(planes[PACK - 1][:, c0 : c0 + width], x_planes[:, PACK - 1, c0 : c0 + width])
            bounds.append((c0, c0 + width, eng))
            c0 = c0 + width
        for i, words in enumerate((w1_words, w2_words, w3_words)):
            nc.sync.dma_start(w_words[i][:].bitcast(I32), words[0].bitcast(I32))

        zeros = keep.tile([P, 2048], BF16, name="zeros", align_bytes=64)
        warm_codes = keep.tile([P, 512], U32, name="warm_codes", align_bytes=64)
        warm_scales = keep.tile([P, 512], U8, name="warm_scales", align_bytes=64)
        warm_bank = psum.tile([P, 512], F32, name="acc2", bufs=3)
        nc.vector.memset(zeros[:], 0.0)
        nc.vector.quantize_mx(out=warm_codes[:].bitcast(FP8X4), scales=warm_scales[:], in_=zeros[:])

        def half_offsets(h):
            return offsets[:, h * (HALF // 16) : (h + 1) * (HALF // 16)]

        for j in range(PACK - 1):
            for h in range(2):
                nc.vector.tensor_copy(grouped[h][:, :, j], planes[j][:].indirect(half_offsets(h)))

        j = PACK - 1
        if SPLIT:
            for a, b, eng in bounds:
                if eng == "s":
                    nc.scalar.activation(last_bf[:, a:b], planes[j][:, a:b], COPY)
                else:
                    nc.vector.tensor_copy(last_bf[:, a:b], planes[j][:, a:b])
        nc.vector.tensor_copy(grouped[0][:, :, j], planes[j][:].indirect(half_offsets(0)))
        if SPLIT:
            nc.scalar.activation(grouped[1][:, :, j], last_bf[:].indirect(half_offsets(1)), COPY)

        units = S // UNIT
        codes = [keep.tile([P, UNIT], U32, name="codes%d" % u, align_bytes=64) for u in range(units)]
        x_scales = [keep.tile([P, UNIT], U8, name="x_scales%d" % u, align_bytes=64) for u in range(units)]
        width = M_TILES * UNIT
        first = keep.tile([P, units * width], F32, name="last_bf")
        pair = keep.tile([P, units * width], F32, name="grouped1", align_bytes=64)
        result = [keep.tile([P, M_TILES, UNIT], F32, name="result%d" % u) for u in range(units)]
        banks = {}

        def quantise(u):
            h, r = divmod(u * UNIT, HALF)
            nc.vector.quantize_mx(
                out=codes[u][:].bitcast(FP8X4),
                scales=x_scales[u][:],
                in_=grouped[h][:, r : r + UNIT, :].rearrange("p n j -> p (n j)"),
            )

        def product(u, i):
            if True:
                acc = psum.tile([P, M_TILES * UNIT], F32, name="acc%d" % i, bufs=(2, 3, 3)[i])
                for mt in range(M_TILES):
                    nc.tensor.matmul_mx(
                        out=acc[:, mt * UNIT : (mt + 1) * UNIT],
                        lhsT=w_words[i][:, 2 * P * mt : 2 * P * (mt + 1)].bitcast(FP4X4),
                        lhsT_scale=w_scales[:, i * N + P * mt : i * N + P * (mt + 1)],
                        rhs=codes[u][:].bitcast(FP8X4),
                        rhs_scale=x_scales[u][:],
                        start=True,
                        stop=True,
                    )
                banks[(u, i)] = acc
            if i == 0:
                nc.scalar.copy(first[:, u * width : (u + 1) * width], banks[(u, 0)][:])

        def min_two(u, lo, hi):
            nc.vector.tensor_tensor(pair[:, u * width + lo * UNIT : u * width + hi * UNIT], banks[(u, 1)][:, lo * UNIT : hi * UNIT], first[:, u * width + lo * UNIT : u * width + hi * UNIT], MIN)

        def min_three(u, lo, hi):
            nc.vector.tensor_tensor(result[u][:, lo:hi, :].rearrange("p m n -> p (m n)"), banks[(u, 2)][:, lo * UNIT : hi * UNIT], pair[:, u * width + lo * UNIT : u * width + hi * UNIT], MIN)
            nc.sync.dma_start(out_view[:, lo:hi, u * UNIT : (u + 1) * UNIT], result[u][:, lo:hi, :])

        for r in range(3):
            nc.tensor.matmul_mx(
                out=warm_bank[:],
                lhsT=w_words[0][:, 0 : 2 * P].bitcast(FP4X4),
                lhsT_scale=w_scales[:, 0:P],
                rhs=warm_codes[:].bitcast(FP8X4),
                rhs_scale=warm_scales[:],
                start=True,
                stop=True,
            )
        quantise(0)
        quantise(1)
        quantise(2)
        quantise(3)
        product(0, 0)
        product(0, 1)
        product(1, 0)
        product(1, 1)
        product(0, 2)
        product(2, 0)
        product(2, 1)
        product(1, 2)
        min_two(0, 0, 2)
        min_two(1, 0, 2)
        product(3, 0)
        product(3, 1)
        product(2, 2)
        min_three(0, 0, 2)
        product(3, 2)
        min_two(2, 0, 2)
        min_three(1, 0, 2)
        min_two(3, 0, 1)
        min_three(2, 0, 1)
        min_two(3, 1, 2)
        min_three(2, 1, 2)
        min_three(3, 0, 1)
        min_three(3, 1, 2)
